import numpy as np
CORES = [6,10,22,26,38,42,54,58]
N = 8
def setup_inputs(rng):
    return {"x": rng.standard_normal((N, 128, 256), dtype=np.float32)}
def reference(x):
    s = x.sum(axis=0, dtype=np.float64).astype(x.dtype)
    s = np.maximum(s, 0)
    return {"y": np.broadcast_to(s, (N,) + s.shape)}

@@ -1,0 +1,67 @@
+from concourse.bass import DstId, RemoteDMATransfer
+from concourse.mybir import AluOpType
+
+SCRATCH = {
+    "xs": ("dram", [8, 128, 32], "float32"),
+    "slots": ("dram", [8, 128, 32], "float32"),
+    "land": ("dram", [8, 128, 32], "float32"),
+    "buf": ("sbuf", [128, 256], "float32"),
+    "res": ("sbuf", [128, 256], "float32"),
+    "zero": ("psum", [128, 256], "float32"),
+}
+SEMAPHORES = ["loaded", "sent", "got", "arrived", "insb", "zset", "relu", "stored"]
+
+
+def rank_program(g, core, T, topo):
+    cores = list(T.cores)
+    n = len(cores)
+    reducers = [c ^ 1 for c in cores]
+    sem = T.sem
+
+    def dst_id(c):
+        rid, pid, _se = topo.addr(c)
+        return DstId(rid=rid, pnc=pid)
+
+    rank = T.rank_of(core)
+    if rank is not None:
+        g.vector.memset(T.zero[:], 0.0).then_inc(sem.zset, 1)
+        g.sync.dma_start(T.xs[:], T.x[:]).then_inc(sem.loaded, 16)
+        g.wait_ge(sem.loaded, 16)
+        transfers = []
+        eng = 0
+        sent = 0
+        for j in range(n):
+            red = reducers[j]
+            if topo.chip(red) == topo.chip(core):
+                m, k = 0xFF00, 8
+            else:
+                m, k = 1 << eng, 1
+                eng += 1
+            sent += k
+            transfers.append(RemoteDMATransfer(dst_ids=[dst_id(red)], dma_engine_mask=m, remote_sem=sem.got,
+                                               srcs=[T.xs[j]], dsts=[T.slots[rank]], alu_op=0))
+        g.remote_dma_fused(transfers, local_sem=sem.sent)
+        g.sync.wait_ge(sem.arrived, 8 * n)
+        g.sync.dma_start(T.buf[:], T.land[:]).then_inc(sem.insb, 16)
+        g.vector.wait_ge(sem.zset, 1)
+        g.vector.wait_ge(sem.insb, 16)
+        g.vector.tensor_tensor(T.res[:], T.buf[:], T.zero[:], AluOpType.max).then_inc(sem.relu, 1)
+        g.sync.wait_ge(sem.relu, 1)
+        g.sync.dma_start(T.y[:], T.res[:]).then_inc(sem.stored, 16)
+        g.wait_ge(sem.sent, sent)
+        g.wait_ge(sem.stored, 16)
+        return
+
+    if core in reducers:
+        j = reducers.index(core)
+        g.wait_ge(sem.got, (n - 1) + 8)
+        srcs = [T.slots[r] for r in range(n)]
+        far = [c for c in cores if topo.chip(c) != topo.chip(core)]
+        near = [c for c in cores if topo.chip(c) == topo.chip(core)]
+        g.remote_dma_fused([
+            RemoteDMATransfer(dst_ids=[dst_id(c) for c in far], dma_engine_mask=0x00FF, remote_sem=sem.arrived,
+                              srcs=srcs, dsts=[T.land[j] for c in far], alu_op=1),
+            RemoteDMATransfer(dst_ids=[dst_id(c) for c in near], dma_engine_mask=0xFF00, remote_sem=sem.arrived,
+                              srcs=srcs, dsts=[T.land[j] for c in near], alu_op=1),
+        ], local_sem=sem.sent)
+        g.wait_ge(sem.sent, 16)

@@ -2,20 +2,21 @@ from concourse.bass import DstId, RemoteDMATransfer
 from concourse.mybir import AluOpType
 
 SCRATCH = {
-    "xs": ("dram", [8, 128, 32], "float32"),
-    "slots": ("dram", [8, 128, 32], "float32"),
-    "land": ("dram", [8, 128, 32], "float32"),
+    "xs": ("dram", [16, 128, 16], "float32"),
+    "slots": ("dram", [8, 128, 16], "float32"),
+    "land": ("dram", [16, 128, 16], "float32"),
     "buf": ("sbuf", [128, 256], "float32"),
     "res": ("sbuf", [128, 256], "float32"),
     "zero": ("psum", [128, 256], "float32"),
 }
-SEMAPHORES = ["loaded", "sent", "got", "arrived", "insb", "zset", "relu", "stored"]
+SEMAPHORES = ["loaded0", "loaded1", "sent", "got", "arrived0", "arrived1", "insb0", "insb1", "zset",
+              "relu0", "relu1", "stored0", "stored1"]
 
 
 def rank_program(g, core, T, topo):
     cores = list(T.cores)
     n = len(cores)
-    reducers = [c ^ 1 for c in cores]
+    reducers = [[c ^ 1 for c in cores], [c ^ 4 for c in cores]]
     sem = T.sem
 
     def dst_id(c):
@@ -24,44 +25,54 @@ def rank_program(g, core, T, topo):
 
     rank = T.rank_of(core)
     if rank is not None:
+        queues = [g.sync, g.scalar]
         g.vector.memset(T.zero[:], 0.0).then_inc(sem.zset, 1)
-        g.sync.dma_start(T.xs[:], T.x[:]).then_inc(sem.loaded, 16)
-        g.wait_ge(sem.loaded, 16)
-        transfers = []
-        eng = 0
+        for h in range(2):
+            queues[h].dma_start(T.xs[8 * h:8 * h + 8], T.x[64 * h:64 * h + 64, :]).then_inc(sem["loaded%d" % h], 16)
         sent = 0
-        for j in range(n):
-            red = reducers[j]
-            if topo.chip(red) == topo.chip(core):
-                m, k = 0xFF00, 8
-            else:
-                m, k = 1 << eng, 1
-                eng += 1
-            sent += k
-            transfers.append(RemoteDMATransfer(dst_ids=[dst_id(red)], dma_engine_mask=m, remote_sem=sem.got,
-                                               srcs=[T.xs[j]], dsts=[T.slots[rank]], alu_op=0))
-        g.remote_dma_fused(transfers, local_sem=sem.sent)
-        g.sync.wait_ge(sem.arrived, 8 * n)
-        g.sync.dma_start(T.buf[:], T.land[:]).then_inc(sem.insb, 16)
+        for h in range(2):
+            g.wait_ge(sem["loaded%d" % h], 16)
+            transfers = []
+            eng = h
+            for j in range(n):
+                red = reducers[h][j]
+                if topo.chip(red) == topo.chip(core):
+                    m, k = 0xFF00, 8
+                else:
+                    m, k = 1 << eng, 1
+                    eng += 1
+                sent += k
+                transfers.append(RemoteDMATransfer(dst_ids=[dst_id(red)], dma_engine_mask=m, remote_sem=sem.got,
+                                                   srcs=[T.xs[8 * h + j]], dsts=[T.slots[rank]], alu_op=0))
+            g.remote_dma_fused(transfers, local_sem=sem.sent)
         g.vector.wait_ge(sem.zset, 1)
-        g.vector.wait_ge(sem.insb, 16)
-        g.vector.tensor_tensor(T.res[:], T.buf[:], T.zero[:], AluOpType.max).then_inc(sem.relu, 1)
-        g.sync.wait_ge(sem.relu, 1)
-        g.sync.dma_start(T.y[:], T.res[:]).then_inc(sem.stored, 16)
+        for h in range(2):
+            q = queues[h]
+            rows = slice(64 * h, 64 * h + 64)
+            q.wait_ge(sem["arrived%d" % h], 8 * n)
+            q.dma_start(T.buf[rows, :], T.land[8 * h:8 * h + 8]).then_inc(sem["insb%d" % h], 16)
+            g.vector.wait_ge(sem["insb%d" % h], 16)
+            g.vector.tensor_tensor(T.res[rows, :], T.buf[rows, :], T.zero[rows, :],
+                                   AluOpType.max).then_inc(sem["relu%d" % h], 1)
+            q.wait_ge(sem["relu%d" % h], 1)
+            q.dma_start(T.y[rows, :], T.res[rows, :]).then_inc(sem["stored%d" % h], 16)
         g.wait_ge(sem.sent, sent)
-        g.wait_ge(sem.stored, 16)
+        g.wait_ge(sem.stored0, 16)
+        g.wait_ge(sem.stored1, 16)
         return
 
-    if core in reducers:
-        j = reducers.index(core)
-        g.wait_ge(sem.got, (n - 1) + 8)
-        srcs = [T.slots[r] for r in range(n)]
-        far = [c for c in cores if topo.chip(c) != topo.chip(core)]
-        near = [c for c in cores if topo.chip(c) == topo.chip(core)]
-        g.remote_dma_fused([
-            RemoteDMATransfer(dst_ids=[dst_id(c) for c in far], dma_engine_mask=0x00FF, remote_sem=sem.arrived,
-                              srcs=srcs, dsts=[T.land[j] for c in far], alu_op=1),
-            RemoteDMATransfer(dst_ids=[dst_id(c) for c in near], dma_engine_mask=0xFF00, remote_sem=sem.arrived,
-                              srcs=srcs, dsts=[T.land[j] for c in near], alu_op=1),
-        ], local_sem=sem.sent)
-        g.wait_ge(sem.sent, 16)
+    for h in range(2):
+        if core in reducers[h]:
+            j = reducers[h].index(core)
+            g.wait_ge(sem.got, (n - 1) + 8)
+            srcs = [T.slots[r] for r in range(n)]
+            far = [c for c in cores if topo.chip(c) != topo.chip(core)]
+            near = [c for c in cores if topo.chip(c) == topo.chip(core)]
+            arrived = sem["arrived%d" % h]
+            g.remote_dma_fused([
+                RemoteDMATransfer(dst_ids=[dst_id(c) for c in far], dma_engine_mask=0x00FF, remote_sem=arrived,
+                                  srcs=srcs, dsts=[T.land[8 * h + j] for c in far], alu_op=1),
+                RemoteDMATransfer(dst_ids=[dst_id(c) for c in near], dma_engine_mask=0xFF00, remote_sem=arrived,
+                                  srcs=srcs, dsts=[T.land[8 * h + j] for c in near], alu_op=1),
+            ], local_sem=sem.sent)
+            g.wait_ge(sem.sent, 16)

@@ -1,22 +1,23 @@
 from concourse.bass import DstId, RemoteDMATransfer
-from concourse.mybir import AluOpType
 
 SCRATCH = {
     "xs": ("dram", [16, 128, 16], "float32"),
     "slots": ("dram", [8, 128, 16], "float32"),
+    "ssum": ("dram", [128, 16], "float32"),
+    "zd": ("dram", [128, 16], "float32"),
+    "zsb": ("sbuf", [128, 16], "float32"),
     "land": ("dram", [16, 128, 16], "float32"),
-    "buf": ("sbuf", [128, 256], "float32"),
-    "res": ("sbuf", [128, 256], "float32"),
-    "zero": ("psum", [128, 256], "float32"),
 }
-SEMAPHORES = ["loaded0", "loaded1", "sent", "got", "arrived0", "arrived1", "insb0", "insb1", "zset",
-              "relu0", "relu1", "stored0", "stored1"]
+SEMAPHORES = ["loaded0", "loaded1", "sent", "got", "summed", "arrived0", "arrived1", "zset", "zdone",
+              "stored0", "stored1"]
+ADD, MAX = 1, 2
 
 
 def rank_program(g, core, T, topo):
     cores = list(T.cores)
     n = len(cores)
-    reducers = [[c ^ 1 for c in cores], [c ^ 4 for c in cores]]
+    spreaders = [[c ^ 4 for c in cores], [c ^ 1 for c in cores]]
+    adders = [[(c >> 2) << 2 for c in spreaders[h]] for h in range(2)]
     sem = T.sem
 
     def dst_id(c):
@@ -26,7 +27,6 @@ def rank_program(g, core, T, topo):
     rank = T.rank_of(core)
     if rank is not None:
         queues = [g.sync, g.scalar]
-        g.vector.memset(T.zero[:], 0.0).then_inc(sem.zset, 1)
         for h in range(2):
             queues[h].dma_start(T.xs[8 * h:8 * h + 8], T.x[64 * h:64 * h + 64, :]).then_inc(sem["loaded%d" % h], 16)
         sent = 0
@@ -35,7 +35,7 @@ def rank_program(g, core, T, topo):
             transfers = []
             eng = h
             for j in range(n):
-                red = reducers[h][j]
+                red = adders[h][j]
                 if topo.chip(red) == topo.chip(core):
                     m, k = 0xFF00, 8
                 else:
@@ -45,34 +45,39 @@ def rank_program(g, core, T, topo):
                 transfers.append(RemoteDMATransfer(dst_ids=[dst_id(red)], dma_engine_mask=m, remote_sem=sem.got,
                                                    srcs=[T.xs[8 * h + j]], dsts=[T.slots[rank]], alu_op=0))
             g.remote_dma_fused(transfers, local_sem=sem.sent)
-        g.vector.wait_ge(sem.zset, 1)
         for h in range(2):
             q = queues[h]
-            rows = slice(64 * h, 64 * h + 64)
             q.wait_ge(sem["arrived%d" % h], 8 * n)
-            q.dma_start(T.buf[rows, :], T.land[8 * h:8 * h + 8]).then_inc(sem["insb%d" % h], 16)
-            g.vector.wait_ge(sem["insb%d" % h], 16)
-            g.vector.tensor_tensor(T.res[rows, :], T.buf[rows, :], T.zero[rows, :],
-                                   AluOpType.max).then_inc(sem["relu%d" % h], 1)
-            q.wait_ge(sem["relu%d" % h], 1)
-            q.dma_start(T.y[rows, :], T.res[rows, :]).then_inc(sem["stored%d" % h], 16)
+            q.dma_start(T.y[64 * h:64 * h + 64, :], T.land[8 * h:8 * h + 8]).then_inc(sem["stored%d" % h], 16)
         g.wait_ge(sem.sent, sent)
         g.wait_ge(sem.stored0, 16)
         g.wait_ge(sem.stored1, 16)
         return
 
     for h in range(2):
-        if core in reducers[h]:
-            j = reducers[h].index(core)
+        if core in adders[h]:
+            j = adders[h].index(core)
             g.wait_ge(sem.got, (n - 1) + 8)
-            srcs = [T.slots[r] for r in range(n)]
+            g.remote_dma_fused([
+                RemoteDMATransfer(dst_ids=[dst_id(spreaders[h][j])], dma_engine_mask=0xFFFF, remote_sem=sem.summed,
+                                  srcs=[T.slots[r] for r in range(n)], dsts=[T.ssum[:]], alu_op=ADD),
+            ], local_sem=sem.sent)
+            g.wait_ge(sem.sent, 16)
+        if core in spreaders[h]:
+            j = spreaders[h].index(core)
+            g.vector.memset(T.zsb[:], 0.0).then_inc(sem.zset, 1)
+            g.sync.wait_ge(sem.zset, 1)
+            g.sync.dma_start(T.zd[:], T.zsb[:]).then_inc(sem.zdone, 16)
+            g.wait_ge(sem.zdone, 16)
+            g.wait_ge(sem.summed, 16)
+            srcs = [T.ssum[:], T.zd[:]]
             far = [c for c in cores if topo.chip(c) != topo.chip(core)]
             near = [c for c in cores if topo.chip(c) == topo.chip(core)]
             arrived = sem["arrived%d" % h]
             g.remote_dma_fused([
                 RemoteDMATransfer(dst_ids=[dst_id(c) for c in far], dma_engine_mask=0x00FF, remote_sem=arrived,
-                                  srcs=srcs, dsts=[T.land[8 * h + j] for c in far], alu_op=1),
+                                  srcs=srcs, dsts=[T.land[8 * h + j] for c in far], alu_op=MAX),
                 RemoteDMATransfer(dst_ids=[dst_id(c) for c in near], dma_engine_mask=0xFF00, remote_sem=arrived,
-                                  srcs=srcs, dsts=[T.land[8 * h + j] for c in near], alu_op=1),
+                                  srcs=srcs, dsts=[T.land[8 * h + j] for c in near], alu_op=MAX),
             ], local_sem=sem.sent)
             g.wait_ge(sem.sent, 16)

@@ -1,23 +1,30 @@
 from concourse.bass import DstId, RemoteDMATransfer
 
+ROW0 = [0, 80, 128]
+WIDTH = [20, 12]
+SPREAD = [4, 1]
+NP = 2
+
 SCRATCH = {
-    "xs": ("dram", [16, 128, 16], "float32"),
-    "slots": ("dram", [8, 128, 16], "float32"),
-    "ssum": ("dram", [128, 16], "float32"),
-    "zd": ("dram", [128, 16], "float32"),
-    "zsb": ("sbuf", [128, 16], "float32"),
-    "land": ("dram", [16, 128, 16], "float32"),
+    "zsb": ("sbuf", [128, 32], "float32"),
 }
-SEMAPHORES = ["loaded0", "loaded1", "sent", "got", "summed", "arrived0", "arrived1", "zset", "zdone",
-              "stored0", "stored1"]
+for _p in range(NP):
+    SCRATCH["xs%d" % _p] = ("dram", [8, 128, WIDTH[_p]], "float32")
+    SCRATCH["land%d" % _p] = ("dram", [8, 128, WIDTH[_p]], "float32")
+    SCRATCH["slots%d" % _p] = ("dram", [8, 128, WIDTH[_p]], "float32")
+    SCRATCH["ssum%d" % _p] = ("dram", [128, WIDTH[_p]], "float32")
+    SCRATCH["zd%d" % _p] = ("dram", [128, WIDTH[_p]], "float32")
+SEMAPHORES = ["sent", "got", "summed", "zset", "zdone"] + [
+    "%s%d" % (s, p) for s in ("loaded", "arrived", "stored") for p in range(NP)]
 ADD, MAX = 1, 2
 
 
 def rank_program(g, core, T, topo):
     cores = list(T.cores)
     n = len(cores)
-    spreaders = [[c ^ 4 for c in cores], [c ^ 1 for c in cores]]
-    adders = [[(c >> 2) << 2 for c in spreaders[h]] for h in range(2)]
+    spread_x = [[c ^ SPREAD[p] for c in cores] for p in range(NP)]
+    adders = [[(c >> 2) << 2 for c in spread_x[p]] for p in range(NP)]
+    spread_y = [[c + 1 for c in adders[p]] for p in range(NP)]
     sem = T.sem
 
     def dst_id(c):
@@ -27,15 +34,15 @@ def rank_program(g, core, T, topo):
     rank = T.rank_of(core)
     if rank is not None:
         queues = [g.sync, g.scalar]
-        for h in range(2):
-            queues[h].dma_start(T.xs[8 * h:8 * h + 8], T.x[64 * h:64 * h + 64, :]).then_inc(sem["loaded%d" % h], 16)
+        for p in range(NP):
+            queues[p].dma_start(T["xs%d" % p][:], T.x[ROW0[p]:ROW0[p + 1], :]).then_inc(sem["loaded%d" % p], 16)
         sent = 0
-        for h in range(2):
-            g.wait_ge(sem["loaded%d" % h], 16)
+        for p in range(NP):
+            g.wait_ge(sem["loaded%d" % p], 16)
             transfers = []
-            eng = h
+            eng = p
             for j in range(n):
-                red = adders[h][j]
+                red = adders[p][j]
                 if topo.chip(red) == topo.chip(core):
                     m, k = 0xFF00, 8
                 else:
@@ -43,41 +50,49 @@ def rank_program(g, core, T, topo):
                     eng += 1
                 sent += k
                 transfers.append(RemoteDMATransfer(dst_ids=[dst_id(red)], dma_engine_mask=m, remote_sem=sem.got,
-                                                   srcs=[T.xs[8 * h + j]], dsts=[T.slots[rank]], alu_op=0))
+                                                   srcs=[T["xs%d" % p][j]], dsts=[T["slots%d" % p][rank]], alu_op=0))
             g.remote_dma_fused(transfers, local_sem=sem.sent)
-        for h in range(2):
-            q = queues[h]
-            q.wait_ge(sem["arrived%d" % h], 8 * n)
-            q.dma_start(T.y[64 * h:64 * h + 64, :], T.land[8 * h:8 * h + 8]).then_inc(sem["stored%d" % h], 16)
+        for p in range(NP):
+            q = queues[p]
+            q.wait_ge(sem["arrived%d" % p], 8 * n)
+            q.dma_start(T.y[ROW0[p]:ROW0[p + 1], :], T["land%d" % p][:]).then_inc(sem["stored%d" % p], 16)
         g.wait_ge(sem.sent, sent)
-        g.wait_ge(sem.stored0, 16)
-        g.wait_ge(sem.stored1, 16)
+        for p in range(NP):
+            g.wait_ge(sem["stored%d" % p], 16)
         return
 
-    for h in range(2):
-        if core in adders[h]:
-            j = adders[h].index(core)
+    for p in range(NP):
+        w = WIDTH[p]
+        if core in adders[p]:
+            j = adders[p].index(core)
             g.wait_ge(sem.got, (n - 1) + 8)
+            two = [spread_x[p][j], spread_y[p][j]]
             g.remote_dma_fused([
-                RemoteDMATransfer(dst_ids=[dst_id(spreaders[h][j])], dma_engine_mask=0xFFFF, remote_sem=sem.summed,
-                                  srcs=[T.slots[r] for r in range(n)], dsts=[T.ssum[:]], alu_op=ADD),
+                RemoteDMATransfer(dst_ids=[dst_id(c) for c in two], dma_engine_mask=0xFFFF, remote_sem=sem.summed,
+                                  srcs=[T["slots%d" % p][r] for r in range(n)],
+                                  dsts=[T["ssum%d" % p][:] for c in two], alu_op=ADD),
             ], local_sem=sem.sent)
             g.wait_ge(sem.sent, 16)
-        if core in spreaders[h]:
-            j = spreaders[h].index(core)
+        if core in spread_x[p] or core in spread_y[p]:
+            is_x = core in spread_x[p]
+            j = spread_x[p].index(core) if is_x else spread_y[p].index(core)
             g.vector.memset(T.zsb[:], 0.0).then_inc(sem.zset, 1)
             g.sync.wait_ge(sem.zset, 1)
-            g.sync.dma_start(T.zd[:], T.zsb[:]).then_inc(sem.zdone, 16)
+            g.sync.dma_start(T["zd%d" % p][:], T.zsb[:, 0:w]).then_inc(sem.zdone, 16)
             g.wait_ge(sem.zdone, 16)
             g.wait_ge(sem.summed, 16)
-            srcs = [T.ssum[:], T.zd[:]]
-            far = [c for c in cores if topo.chip(c) != topo.chip(core)]
-            near = [c for c in cores if topo.chip(c) == topo.chip(core)]
-            arrived = sem["arrived%d" % h]
-            g.remote_dma_fused([
-                RemoteDMATransfer(dst_ids=[dst_id(c) for c in far], dma_engine_mask=0x00FF, remote_sem=arrived,
-                                  srcs=srcs, dsts=[T.land[8 * h + j] for c in far], alu_op=MAX),
-                RemoteDMATransfer(dst_ids=[dst_id(c) for c in near], dma_engine_mask=0xFF00, remote_sem=arrived,
-                                  srcs=srcs, dsts=[T.land[8 * h + j] for c in near], alu_op=MAX),
-            ], local_sem=sem.sent)
-            g.wait_ge(sem.sent, 16)
+            srcs = [T["ssum%d" % p][:], T["zd%d" % p][:]]
+            par = topo.chip(core) & 1
+            mine = [c for c in cores if ((topo.chip(c) & 1) != par) == is_x]
+            far = [c for c in mine if topo.chip(c) != topo.chip(core)]
+            near = [c for c in mine if topo.chip(c) == topo.chip(core)]
+            arrived = sem["arrived%d" % p]
+            land = T["land%d" % p]
+            transfers = [RemoteDMATransfer(dst_ids=[dst_id(c) for c in far], dma_engine_mask=0x00FF,
+                                           remote_sem=arrived, srcs=srcs, dsts=[land[j] for c in far], alu_op=MAX)]
+            if near:
+                transfers.append(RemoteDMATransfer(dst_ids=[dst_id(c) for c in near], dma_engine_mask=0xFF00,
+                                                   remote_sem=arrived, srcs=srcs, dsts=[land[j] for c in near],
+                                                   alu_op=MAX))
+            g.remote_dma_fused(transfers, local_sem=sem.sent)
+            g.wait_ge(sem.sent, 8 * len(transfers))

from concourse.bass import DstId, RemoteDMATransfer

ROW0 = [0, 80, 128]
WIDTH = [20, 12]
SPREAD = [4, 1]
NP = 2

SCRATCH = {
    "zsb": ("sbuf", [128, 32], "float32"),
}
for _p in range(NP):
    SCRATCH["xs%d" % _p] = ("dram", [8, 128, WIDTH[_p]], "float32")
    SCRATCH["land%d" % _p] = ("dram", [8, 128, WIDTH[_p]], "float32")
    SCRATCH["slots%d" % _p] = ("dram", [8, 128, WIDTH[_p]], "float32")
    SCRATCH["ssum%d" % _p] = ("dram", [128, WIDTH[_p]], "float32")
    SCRATCH["zd%d" % _p] = ("dram", [128, WIDTH[_p]], "float32")
SEMAPHORES = ["sent", "got", "summed", "zset", "zdone"] + [
    "%s%d" % (s, p) for s in ("loaded", "arrived", "stored") for p in range(NP)]
ADD, MAX = 1, 2


def rank_program(g, core, T, topo):
    cores = list(T.cores)
    n = len(cores)
    spread_x = [[c ^ SPREAD[p] for c in cores] for p in range(NP)]
    adders = [[(c >> 2) << 2 for c in spread_x[p]] for p in range(NP)]
    spread_y = [[c + 1 for c in adders[p]] for p in range(NP)]
    sem = T.sem

    def dst_id(c):
        rid, pid, _se = topo.addr(c)
        return DstId(rid=rid, pnc=pid)

    rank = T.rank_of(core)
    if rank is not None:
        queues = [g.sync, g.scalar]
        for p in range(NP):
            queues[p].dma_start(T["xs%d" % p][:], T.x[ROW0[p]:ROW0[p + 1], :]).then_inc(sem["loaded%d" % p], 16)
        sent = 0
        for p in range(NP):
            g.wait_ge(sem["loaded%d" % p], 16)
            transfers = []
            eng = p
            for j in range(n):
                red = adders[p][j]
                if topo.chip(red) == topo.chip(core):
                    m, k = 0xFF00, 8
                else:
                    m, k = 1 << eng, 1
                    eng += 1
                sent += k
                transfers.append(RemoteDMATransfer(dst_ids=[dst_id(red)], dma_engine_mask=m, remote_sem=sem.got,
                                                   srcs=[T["xs%d" % p][j]], dsts=[T["slots%d" % p][rank]], alu_op=0))
            g.remote_dma_fused(transfers, local_sem=sem.sent)
        for p in range(NP):
            q = queues[p]
            q.wait_ge(sem["arrived%d" % p], 8 * n)
            q.dma_start(T.y[ROW0[p]:ROW0[p + 1], :], T["land%d" % p][:]).then_inc(sem["stored%d" % p], 16)
        g.wait_ge(sem.sent, sent)
        for p in range(NP):
            g.wait_ge(sem["stored%d" % p], 16)
        return

    for p in range(NP):
        w = WIDTH[p]
        if core in adders[p]:
            j = adders[p].index(core)
            g.wait_ge(sem.got, (n - 1) + 8)
            two = [spread_x[p][j], spread_y[p][j]]
            g.remote_dma_fused([
                RemoteDMATransfer(dst_ids=[dst_id(c) for c in two], dma_engine_mask=0xFFFF, remote_sem=sem.summed,
                                  srcs=[T["slots%d" % p][r] for r in range(n)],
                                  dsts=[T["ssum%d" % p][:] for c in two], alu_op=ADD),
            ], local_sem=sem.sent)
            g.wait_ge(sem.sent, 16)
        if core in spread_x[p] or core in spread_y[p]:
            is_x = core in spread_x[p]
            j = spread_x[p].index(core) if is_x else spread_y[p].index(core)
            g.vector.memset(T.zsb[:], 0.0).then_inc(sem.zset, 1)
            g.sync.wait_ge(sem.zset, 1)
            g.sync.dma_start(T["zd%d" % p][:], T.zsb[:, 0:w]).then_inc(sem.zdone, 16)
            g.wait_ge(sem.zdone, 16)
            g.wait_ge(sem.summed, 16)
            srcs = [T["ssum%d" % p][:], T["zd%d" % p][:]]
            par = topo.chip(core) & 1
            mine = [c for c in cores if ((topo.chip(c) & 1) != par) == is_x]
            far = [c for c in mine if topo.chip(c) != topo.chip(core)]
            near = [c for c in mine if topo.chip(c) == topo.chip(core)]
            arrived = sem["arrived%d" % p]
            land = T["land%d" % p]
            transfers = [RemoteDMATransfer(dst_ids=[dst_id(c) for c in far], dma_engine_mask=0x00FF,
                                           remote_sem=arrived, srcs=srcs, dsts=[land[j] for c in far], alu_op=MAX)]
            if near:
                transfers.append(RemoteDMATransfer(dst_ids=[dst_id(c) for c in near], dma_engine_mask=0xFF00,
                                                   remote_sem=arrived, srcs=srcs, dsts=[land[j] for c in near],
                                                   alu_op=MAX))
            g.remote_dma_fused(transfers, local_sem=sem.sent)
            g.wait_ge(sem.sent, 8 * len(transfers))
